import numpy as np, ml_dtypes
CORES = [9,25,41,57]
N = 4
BF = ml_dtypes.bfloat16
def gentries(a):
    return np.ascontiguousarray(a.reshape(8, 16, -1).transpose(0, 2, 1)).reshape(8, -1)
def gtable(e):
    e = np.asarray(e); return np.ascontiguousarray(e.reshape(8, -1, 16).transpose(0, 2, 1)).reshape(128, -1).astype(np.int32)
S, Q, T, CAP, RO = 2048, 4, 256, 128, 4
B = Q * S
def near(rng, c, a):
    return np.clip(np.take_along_axis(c, a[:, :, None, :], 3) + rng.integers(-40, 41, (N, 8, 16, T)), 0, 255)
def parts(rng):
    c = rng.integers(0, 256, (N, 8, 16, S)); g = rng.integers(-16, 16, (N, 8, 16, B))
    H = S >> 4; hub = np.argsort(rng.random((N, 8, S)), axis=2)[..., :H]
    i = np.minimum((H * rng.random((N, 8, 16 * S)) ** 2).astype(np.int64), H - 1)
    u = np.take_along_axis(hub, i, 2).reshape(N, 8, 16, S); u = np.where(rng.random(u.shape) < 0.5, u, rng.integers(0, S, u.shape))
    i = np.minimum((H * rng.random((N, 8, T)) ** 2).astype(np.int64), H - 1)
    a = np.take_along_axis(hub, i, 2); a = np.where(rng.random(a.shape) < 0.5, a, rng.integers(0, S, a.shape))
    h = rng.integers(0, Q, (N, 8, S)); e = rng.choice(np.array([0.1, 0.3, 0.6]), (N, 8, 1))
    f = np.where(rng.random((N, 8, S)) < e, 0, rng.integers(0, Q + 1, (N, 8, S)))
    return c, u, g, h, f, a, near(rng, c, a)
def pack(c, u, g, h, f, a, z):
    return {"xs": np.ascontiguousarray(c.reshape(N, 128, S)).astype(np.float32).astype(BF), "su": np.ascontiguousarray(u.reshape(N, 128, S)).astype(np.int32),
            "gs": np.ascontiguousarray(g.reshape(N, 128, B)).astype(np.float32).astype(BF), "hd0": h.astype(np.int32), "fl0": f.astype(np.int32),
            "a0": np.stack([gtable(v) for v in a]), "z0": np.ascontiguousarray(z.reshape(N, 128, T)).astype(np.float32).astype(BF)}
def setup_inputs(rng):
    return pack(*parts(rng))
def setup_inputs_room(rng):
    c, u, g, h, f, a, z = parts(rng); num = (CAP, CAP + 1, T, CAP - 1, 1, 0, CAP, CAP + 1)
    for r in range(N):
        for k in range(8):
            j = (r + k) % 8; o = rng.permutation(S)[:T]; a[r, k] = o
            full = rng.integers(1, Q + 1, T)
            if j in (3, 5, 6):
                full[:] = 1 if j == 5 else Q
                u[r, k] = np.arange(S)
            f[r, k, o] = np.where(rng.permutation(T) < num[j], 0, full)
    return pack(c, u, g, h, f, a, near(rng, c, a))
def setup_inputs_crowd(rng):
    c, u, g, h, f, a, z = parts(rng)
    for r in range(N):
        for k in range(8):
            j = (r + k) % 8
            if j == 7: continue
            o = np.concatenate([rng.permutation(np.array([0, S - 1])), 1 + rng.permutation(S - 2)])
            if j < 4:
                n = (1, 2, 5, 12)[j]; a[r, k] = o[rng.integers(0, n, T)]; u[r, k] = o[rng.integers(0, n, (16, S))]
            else:
                w = (Q, Q, Q + 1)[j - 4]; o = o[:(T + w - 1) // w]
                a[r, k] = rng.permutation(np.repeat(o, w)[:T]); f[r, k, o] = (Q, 0, 0)[j - 4]
    return pack(c, u, g, h, f, a, near(rng, c, a))
def setup_inputs_ties(rng):
    c, u, g, h, f, a, z = parts(rng); pro = rng.integers(2, 254, (8, 16, 3))
    for k in range(8):
        if k % 2 == 0:
            c[:, k] = pro[k][:, np.arange(S) % 3]; g[:, k] = 2 * rng.integers(0, 2, (N, 16, B)) - 1; f[:, k] = f[:, k] * (rng.random((N, S)) < 0.5)
            if k % 4 == 2:
                g[:, k] = g[:, k] * rng.integers(0, 2, (N, 1, B)); u[:, k, 0] = np.where(rng.random((N, S)) < 0.5, np.arange(S), u[:, k, 0])
        else:
            c[:, k] = c[:, k][..., np.arange(S) // 2 * 2]; g[:, k] = g[:, k][..., np.arange(B) & 31]
    z = near(rng, c, a); z[:, ::2] = np.take_along_axis(c[:, ::2], a[:, ::2, None, :], 3)
    return pack(c, u, g, h, f, a, z)
def setup_inputs_ends(rng):
    c, u, g, h, f, a, z = parts(rng)
    c = 255 * rng.integers(0, 2, c.shape); g = 31 * rng.integers(0, 2, g.shape) - 16; z = 255 * rng.integers(0, 2, z.shape)
    k = rng.integers(0, 3, (N, 8, 1, T)); z = np.where(k == 0, 0, np.where(k == 1, 255, z))
    p = rng.permutation(8)
    f[:, p[0]] = 0; f[:, p[1]] = Q; h[:, p[2]] = Q - 1; h[:, p[3]] = 0
    for j in (4, 5, 6):
        w = p[j]; cw = rng.integers(0, 2, (N, 16, S)); zw = 255 - rng.integers(0, 2, (N, 16, T)); f[:, w] = Q * rng.integers(0, 2, (N, S))
        if j < 6:
            two = np.argsort(rng.random((N, 16, B)), axis=1) < 2
            gw = np.where(two, -rng.integers(1, 9, (N, 16, B)), rng.integers(6, 16, (N, 16, B)))
            if j == 5: cw = 255 - cw; zw = 255 - zw; gw = -gw
            g[:, w] = gw
        c[:, w] = cw; z[:, w] = zw
    a[..., 0] = 0; a[..., 1] = S - 1; a[..., T - 2] = 0; a[..., T - 1] = S - 1
    u = np.where(rng.random(u.shape) < 0.3, (S - 1) * rng.integers(0, 2, u.shape), u)
    return pack(c, u, g, h, f, a, z)
def setup_inputs_spread(rng):
    c, u, g, h, f, a, z = parts(rng)
    c = np.minimum((256 * rng.random(c.shape) ** np.exp2(rng.uniform(-3, 3, (N, 8, 1, S)))).astype(np.int64), 255)
    z = np.minimum((256 * rng.random(z.shape) ** np.exp2(rng.uniform(-3, 3, (N, 8, 1, T)))).astype(np.int64), 255)
    g = np.clip(np.floor((rng.random(g.shape) * 2 - 1) * np.exp2(rng.uniform(-2, 4, (N, 8, 1, B)))).astype(np.int64), -16, 15)
    m = rng.permuted(np.tile(np.arange(S), (N, 8, 1)), axis=2)
    i = np.minimum((S * rng.random((N, 8, 16 * S)) ** rng.uniform(1, 5, (N, 8, 1))).astype(np.int64), S - 1); u = np.take_along_axis(m, i, 2).reshape(N, 8, 16, S)
    i = np.minimum((S * rng.random((N, 8, T)) ** rng.uniform(1, 5, (N, 8, 1))).astype(np.int64), S - 1); a = np.take_along_axis(m, i, 2)
    f = np.minimum(((Q + 1) * rng.random((N, 8, S)) ** np.exp2(rng.uniform(-2, 2, (N, 8, 1)))).astype(np.int64), Q)
    return pack(c, u, g, h, f, a, z)
def check_inputs(d):
    bad = []
    for k, lo, hi in (("xs", 0, 255), ("su", 0, S - 1), ("gs", -16, 15), ("hd0", 0, Q - 1), ("fl0", 0, Q), ("a0", 0, S - 1), ("z0", 0, 255)):
        v = np.asarray(d[k]).astype(np.float64)
        if not (np.all(v >= lo) and np.all(v <= hi) and np.all(v == np.floor(v))): bad.append("range of " + k)
    return bad
def reference(xs, su, gs, hd0, fl0, a0, z0):
    X = xs.astype(np.float32).astype(np.int64).reshape(N, 8, 16, S); U = su.astype(np.int64).reshape(N, 8, 16, S)
    G = gs.astype(np.float32).astype(np.int64).reshape(N, 8, 16, B); hd = hd0.astype(np.int64); fl = fl0.astype(np.int64)
    a = np.stack([gentries(v) for v in a0]).astype(np.int64); z = z0.astype(np.float32).astype(np.int64).reshape(N, 8, 16, T)
    low = np.tri(T, k=-1, dtype=bool); odd = 2 * np.arange(16)[:, None] + 1
    for t in range(RO):
        same = a[:, :, :, None] == a[:, :, None, :]
        place = np.sum(same & low, axis=3); count = np.sum(same, axis=3)
        ha = np.take_along_axis(hd, a, 2); fa = np.take_along_axis(fl, a, 2)
        pop = place < fa; slot = Q * a + ((ha + place) & (Q - 1))
        zn = np.clip(z + np.take_along_axis(G, slot[:, :, None, :], 3), 0, 255)
        s = np.take_along_axis(U, a[:, :, None, :], 3)
        c = np.take_along_axis(X, s.reshape(N, 8, 1, 16 * T), 3).reshape(N, 8, 16, 16, T)
        best = np.argmin(np.sum(np.abs(c - zn[:, :, :, None, :]), axis=2), axis=2)
        to = np.take_along_axis(s, best[:, :, None, :], 2)[:, :, 0]
        gone = np.minimum(count, fa)
        np.put_along_axis(hd, a, (ha + gone) & (Q - 1), 2); np.put_along_axis(fl, a, fa - gone, 2)
        ask = ~pop & (np.add.accumulate((~pop).astype(np.int64), axis=2) <= CAP)
        d = 1 + t % (N - 1); XR = np.roll(X, -d, axis=0); GR = np.roll(G, -d, axis=0)
        u = np.sum(odd * z, axis=2) & 4095
        ix = (((u * u) >> 5)[:, :, None, :] + odd * u[:, :, None, :]) & (B - 1)
        cand = np.take_along_axis(GR, ix.reshape(N, 8, 1, 16 * T), 3).reshape(N, 8, 16, 16, T)
        goal = np.take_along_axis(XR, a[:, :, None, :], 3)
        m = np.argmin(np.sum(np.abs(z[:, :, :, None, :] + cand - goal[:, :, :, None, :]), axis=2), axis=2)
        seg = np.take_along_axis(cand, m[:, :, None, None, :], 3)[:, :, :, 0]
        put = ask & (place - fa < Q)
        for r in range(N):
            for g in range(8):
                w = np.flatnonzero(put[r, g])
                G[r, g][:, slot[r, g, w]] = seg[r, g][:, w]
                np.add.at(fl[r, g], a[r, g, w], 1)
        a = np.where(pop, to, a); z = np.where(pop[:, :, None, :], zn, z)
    return {"yz": z.reshape(N, 128, T).astype(np.float32).astype(BF), "ya": a.astype(np.float32), "yh": hd.astype(np.float32), "yf": fl.astype(np.float32)}

@@ -1,0 +1,509 @@
+from concourse.mybir import AluOpType as Op, ActivationFunctionType as Fn
+
+STEPS = 4
+ASKS = STEPS - 1
+B0, BD, BE = 16, 8208, 8336
+PSUM = ["ps%d" % i for i in range(8)]
+SCRATCH = {}
+for _n in PSUM:
+    SCRATCH[_n] = ("psum", [128, 512], "float32")
+WIDE = {"xw": (2048, "bfloat16"), "sui": (4096, "int32"), "bank": (BE, "bfloat16"), "hm": (2048, "bfloat16"), "cc": (4096, "bfloat16"),
+        "mx": (4096, "bfloat16"), "cand": (2048, "bfloat16"), "mq": (2048, "bfloat16"), "eb": (4096, "bfloat16"), "lh": (2048, "bfloat16"),
+        "rh": (2048, "bfloat16"), "rd": (2048, "bfloat16"), "za": (256, "bfloat16"), "zb": (256, "bfloat16")}
+for _n, (_w, _d) in WIDE.items():
+    SCRATCH[_n] = ("sbuf", [128, _w], _d)
+NARROW = {
+    "float32": "pcol 1 p16 1 pdiv 1 odd 1 l16 1 ge8 1 is0 1 jf 256 pat16 256 patc8 128 mask16 256 qd16 128 gm 64 rpt 128 cw 128 cwt 128 e8f 8 dump 8 dump2 8 "
+               "als 16 al4 16 alof 16 ahif 16 arm 256 gc_ 256 b4 16 d1 16 s1 16 s2 16 y1 16 p8 16 yv 16 oq 16 pp 16 sb 16 pt 16 wl 16 ks 256 ko 128 k1 128 "
+               "k2 64 k3 32 k4 16 arf 256 pv1 16 pv2 16 pv3 16 pv 16 ca 256 cb 128 cb2 128 cm 64 c1 32 c2 16 v2 8 v3 8 v4 8 um 128 q0 64 q1 64 q2 32 q3 16 "
+               "q6 8 ohf 128 oyf 128",
+    "int32": "ci 1 ci2 1 ci3 1 ji 256 jt 256 hi0 128 fi0 128 a0i 16 ai 16 alo 16 ahi 16 cdi 16 hh 16 tl 16 xx 16 x3 16 ri 16 rlo 16 rhi 16 lni 8 v1 8 qa 8 "
+             "ui 128 uu 128 usq 128 uv 128 us 128 ux 128 q4 8 q5 8 w1 128 w2 128 w3 128 w4 128",
+    "uint16": "e16 16 e8 8 alu 16 alou 16 suu 256 offu 16 sou 16 lnu 8 qau 8 cou 128 seu 8",
+    "bfloat16": "bo 128 bow 128 ob8 8 o32 8 om16 8 idb 128 idn 128 tri 128 ones 128 rp 128 i128 128 maskm 256 lanb 16 rowc 256 dg 256 blk 16 ay 256 "
+                "zs 256 oh 256 goal 128",
+    "float16": "boh 128 ob8h 8 ob8k 8 arow 256 os 256 gmk 256 sp 256 aa 256 aq 128"}
+PACK = {}
+for _d, _t in NARROW.items():
+    _at, _f = 0, _t.split()
+    for _n, _w in zip(_f[::2], _f[1::2]):
+        PACK[_n] = ("pk_" + _d, _at, int(_w))
+        _at += -(-int(_w) // 16) * 16
+    SCRATCH["pk_" + _d] = ("sbuf", [128, _at], _d)
+for _t in range(ASKS):
+    for _n, _w, _d in (("qp", 8, "int32"), ("zq", 128, "bfloat16"), ("an", 128, "bfloat16"),
+                       ("qpin", 8, "int32"), ("zqin", 128, "bfloat16"), ("anin", 128, "bfloat16"), ("offr", 8, "uint16")):
+        SCRATCH["%s%d" % (_n, _t)] = ("sbuf", [128, _w], _d)
+LOADS = ["la", "ls", "lx", "lh0", "lf0", "lz", "lg"]
+SEMAPHORES = ["sv", "ss", "st", "sg", "sent", "sout"] + LOADS + ["%s%d" % (n, t) for t in range(ASKS) for n in ("rp", "rz", "ra")]
+
+
+def rank_program(g, core, T, topo):
+    rank = T.rank_of(core)
+    if rank is None:
+        return
+    N = len(T.cores)
+    qobj = {"v": g.vector, "s": g.scalar, "t": g.tensor, "g": g, "d": g.sync}
+    qsem = {"v": "sv", "s": "ss", "t": "st", "g": "sg"}
+    count = {"v": 0, "s": 0, "t": 0, "g": 0}
+    known = {q: {} for q in qobj}
+    recs = {}
+
+    def need(q, sem, n, snap):
+        kn = known[q]
+        if kn.get(sem, 0) < n:
+            qobj[q].wait_ge(T.sem[sem], n)
+            kn[sem] = n
+            for a, b in snap.items():
+                if kn.get(a, 0) < b:
+                    kn[a] = b
+
+    def access(q, reads, writes):
+        todo = {}
+        for wr, refs in ((False, reads), (True, writes)):
+            for name, lo, hi in refs:
+                for r in recs.get(name, ()):
+                    hit = r[3] != q if name in PSUM else r[0] < hi and lo < r[1] and (r[2] or wr)
+                    if hit and (r[4] not in todo or todo[r[4]][0] < r[5]):
+                        todo[r[4]] = (r[5], r[6])
+        for sem in sorted(todo, key=lambda s: -len(todo[s][1])):
+            need(q, sem, todo[sem][0], todo[sem][1])
+
+    def note(q, sem, n, reads, writes):
+        snap = dict(known[q])
+        for wr, refs in ((False, reads), (True, writes)):
+            for name, lo, hi in refs:
+                old = recs.get(name, [])
+                if name in PSUM:
+                    old = [r for r in old if r[3] != q]
+                elif wr:
+                    old = [r for r in old if not (lo <= r[0] and r[1] <= hi)]
+                else:
+                    old = [r for r in old if r[2] or r[3] != q or not (lo <= r[0] and r[1] <= hi)]
+                old.append((lo, hi, wr, q, sem, n, snap))
+                recs[name] = old
+
+    def op(q, out, ins, emit):
+        reads = [x for r in ins for x in r[1]]
+        access(q, reads, out[1])
+        count[q] += 1
+        emit(qobj[q]).then_inc(T.sem[qsem[q]], 1)
+        note(q, qsem[q], count[q], reads, out[1])
+
+    def R(name, a=0, b=None, st=1):
+        buf, base, w = PACK[name] if name in PACK else (name, 0, SCRATCH[name][1][1])
+        b = w if b is None else b
+        ap = T[buf][:, base + a:base + b] if st == 1 else T[buf][:, base + a:base + b:st]
+        return (ap, [(buf, base + a, base + b)])
+
+    def IND(win, off):
+        return (win[0].indirect(off[0]), win[1] + off[1])
+
+    def sc(x):
+        return x[0] if isinstance(x, tuple) else x
+
+    def tc(out, a):
+        op("v", out, [a], lambda e: e.tensor_copy(out[0], a[0]))
+
+    def tt(out, a, b, o):
+        op("v", out, [a, b], lambda e: e.tensor_tensor(out[0], a[0], b[0], o))
+
+    def ts(out, a, s1, o1, s2=None, o2=None):
+        ins = [a] + [s for s in (s1, s2) if isinstance(s, tuple)]
+        if o2 is None:
+            op("v", out, ins, lambda e: e.tensor_scalar(out[0], a[0], sc(s1), None, o1))
+        else:
+            op("v", out, ins, lambda e: e.tensor_scalar(out[0], a[0], sc(s1), sc(s2), o1, o2))
+
+    def act(out, a):
+        op("s", out, [a], lambda e: e.activation(out[0], a[0], Fn.Copy))
+
+    def actf(out, a, fn, bias, scale):
+        ins = [a] + [s for s in (bias, scale) if isinstance(s, tuple)]
+        op("s", out, ins, lambda e: e.activation(out[0], a[0], fn, bias=sc(bias), scale=sc(scale)))
+
+    def mm(out, l, r, start=True, stop=True):
+        op("t", out, [l, r], lambda e: e.matmul(out[0], l[0], r[0], start, stop))
+
+    def iota(out, pattern, cm):
+        op("g", out, [], lambda e: e.iota(out[0], pattern, 0, cm))
+
+    def fill(out, c):
+        op("v", out, [], lambda e: e.memset(out[0], c))
+
+    def landed(ref, q, sem, n):
+        for name, lo, hi in ref[1]:
+            recs.setdefault(name, []).append((lo, hi, True, q, sem, n, {}))
+
+    def load(out, src, sem):
+        g.sync.dma_start(out[0], src).then_inc(T.sem[sem], 16)
+        landed(out, "dma", sem, 16)
+
+    sends = [0]
+
+    def send(to, out, src, sem):
+        dst = T.cores[to]
+        rid, pid = topo.addr(dst)[:2]
+        access("g", src[1], [])
+        g.remote_dma(out[0], src[0], T.sem[sem], T.sem["sent"], pid, rid, topo.mask(core, dst))
+        sends[0] += len(topo.engines(core, dst))
+
+    load(R("a0i"), T.a0[:, :], "la")
+    load(R("hi0"), T.hd0[:, :], "lh0")
+    load(R("fi0"), T.fl0[:, :], "lf0")
+    load(R("sui", 0, 2048), T.su[:, :], "ls")
+    load(R("xw"), T.xs[:, :], "lx")
+    load(R("za"), T.z0[:, :], "lz")
+    load(R("bank", B0, BD), T.gs[:, :], "lg")
+    arrive = {}
+    for t in range(ASKS):
+        asker, asked = T.cores[(rank - 1 - t % (N - 1)) % N], T.cores[(rank + 1 + t % (N - 1)) % N]
+        for n, sem, src in (("qpin", "rp", asker), ("zqin", "rz", asker), ("anin", "ra", asked)):
+            arrive["%s%d" % (sem, t)] = len(topo.engines(src, core))
+            landed(R("%s%d" % (n, t)), "rem", "%s%d" % (sem, t), len(topo.engines(src, core)))
+
+    iota(R("ci"), [[1, 1]], 1)
+    iota(R("ji"), [[1, 256]], 0)
+    iota(R("sui", 2048, 4096), [[1, 2048]], 0)
+    tc(R("pcol"), R("ci"))
+    tc(R("jf"), R("ji"))
+    ts(R("ci2"), R("ci"), 15, Op.bitwise_and)
+    ts(R("ci3"), R("ci"), 4, Op.arith_shift_right)
+    tc(R("p16"), R("ci2"))
+    tc(R("pdiv"), R("ci3"))
+    ts(R("jt"), R("ji"), 15, Op.bitwise_and)
+    tc(R("pat16"), R("jt"))
+    ts(R("mask16"), R("pat16"), R("p16"), Op.is_equal)
+    tc(R("e16"), R("ji", 0, 16))
+    ts(R("jt", 0, 128), R("ji", 0, 128), 4, Op.arith_shift_right)
+    tc(R("qd16"), R("jt", 0, 128))
+    ts(R("boh"), R("qd16"), R("pdiv"), Op.is_equal)
+    ts(R("ob8h"), R("jf", 0, 8), R("pdiv"), Op.is_equal)
+    ts(R("ob8k"), R("ob8h"), 1024.0, Op.mult)
+    ts(R("maskm"), R("pat16"), R("p16"), Op.is_le, 4096.0, Op.mult)
+    ts(R("bo"), R("qd16"), R("pdiv"), Op.is_equal)
+    ts(R("ob8"), R("jf", 0, 8), R("pdiv"), Op.is_equal)
+    ts(R("idb"), R("jf", 0, 128), R("pcol"), Op.is_equal)
+    ts(R("lanb", 0, 8), R("jf", 0, 8), 0.0, Op.mult, R("pcol"), Op.add)
+    ts(R("lanb", 8, 16), R("lanb", 0, 8), 128.0, Op.add)
+    fill(R("ones"), 1.0)
+    for j in range(16):
+        actf(R("hm", 128 * j, 128 * j + 128), R("ones"), Fn.Copy, 0.0, R("mask16", j, j + 1))
+    tc(R("als"), R("a0i"))
+    tt(R("os"), IND(R("als"), R("e16")), R("mask16"), Op.mult)
+
+    def spread(t):
+        mm(R("ps1", 0, 256), R("boh"), R("os"))
+        if t < STEPS:
+            mm(R("ps3", 256, 512), R("boh"), R("os"), True, False)
+            mm(R("ps3", 256, 512), R("idb"), R("maskm"), False, True)
+            act(R("arm"), R("ps3", 256, 512))
+        if t < ASKS:
+            for h in (0, 1):
+                o = R("ps1", 272 + 8 * h, 280 + 8 * h)
+                mm(o, R("os", 128 * h, 128 * h + 128), R("ob8k"), True, False)
+                mm(o, R("idb"), R("lanb", 8 * h, 8 * h + 8), False, True)
+
+    spread(0)
+    fill(R("eb"), 0.0)
+    fill(R("bank", 0, B0), 0.0)
+    ts(R("idn"), R("idb"), -1.0, Op.mult)
+    ts(R("rpt"), R("idb"), 512.0, Op.mult)
+    ts(R("cwt"), R("jf", 0, 128), R("pcol"), Op.is_gt)
+    tt(R("tri"), R("cwt"), R("rpt"), Op.subtract)
+    ts(R("i128"), R("jf", 0, 128), 0.0, Op.add)
+    ts(R("rpt"), R("pat16", 0, 128), 1.0, Op.add)
+    tt(R("rpt"), R("rpt"), R("bo"), Op.mult)
+    ts(R("rp"), R("rpt"), -1.0, Op.add)
+    ts(R("o32"), R("ob8"), 32.0, Op.mult)
+    ts(R("om16"), R("ob8"), -16.0, Op.mult)
+    ts(R("odd"), R("p16"), 2.0, Op.mult, 1.0, Op.add)
+    ts(R("bow"), R("bo"), R("odd"), Op.mult)
+    ts(R("l16"), R("pcol"), 16.0, Op.mult)
+    ts(R("ge8"), R("p16"), 8.0, Op.is_ge)
+    ts(R("e8f"), R("jf", 0, 8), 2.0, Op.mult, R("ge8"), Op.add)
+    tc(R("e8"), R("e8f"))
+    ts(R("jt", 0, 128), R("ji", 0, 128), 7, Op.bitwise_and)
+    ts(R("patc8"), R("jt", 0, 128), -32.0, Op.add)
+    ts(R("jt", 0, 64), R("ji", 0, 64), 3, Op.arith_shift_right)
+    ts(R("gm"), R("jt", 0, 64), R("pdiv"), Op.is_equal)
+    ts(R("dump"), R("jf", 0, 8), 16.0, Op.mult, R("p16"), Op.add)
+    ts(R("dump2"), R("dump"), float(BD + 8192 - B0), Op.add)
+    ts(R("dump"), R("dump"), float(BD), Op.add)
+    ts(R("is0"), R("pcol"), 0.0, Op.is_equal)
+    ts(R("rowc"), R("pat16"), R("is0"), Op.mult)
+    ts(R("cwt"), R("hi0"), 33.0, Op.mult)
+    ts(R("cw"), R("fi0"), 32.0, Op.mult)
+    tt(R("cw"), R("cw"), R("cwt"), Op.add)
+
+    z = ["za", "zb"]
+
+    def head(t):
+        tc(R("ai"), R("als"))
+        tc(R("alu"), R("als"))
+        ts(R("alo"), R("ai"), 127, Op.bitwise_and)
+        tc(R("suu"), IND(R("sui", 0, 2048), R("alu")))
+        tc(R("alou"), R("alo"))
+        if t > 0:
+            act(R("gc_"), IND(R("cw"), R("alou")))
+        for k in range(4):
+            act(R("cc", 1024 * k, 1024 * k + 1024), IND(R("xw"), R("suu", 64 * k, 64 * k + 64)))
+            if t == 0 and k == 1:
+                act(R("gc_"), IND(R("cw"), R("alou")))
+        yield
+        tc(R("arow"), R("ps1", 0, 256))
+        yield
+        for c in range(15):
+            ts(R("eb", 272 * c + 16, 256 * c + 256), R("arow", 16 * c + 16, 256), R("als", c, c + 1), Op.is_equal)
+            yield
+        tt(R("dg"), IND(R("als"), R("e16")), R("arm"), Op.is_equal)
+        for h in (0, 1):
+            for c in range(7 if h == 0 else 15):
+                mm(R("ps2", 8 * h, 8 * h + 8), R("eb", 256 * c + 128 * h, 256 * c + 128 * h + 128), R("ob8"), c == 0, False)
+            mm(R("ps2", 8 * h, 8 * h + 8), R("dg", 128 * h, 128 * h + 128), R("ob8"), False, True)
+        yield
+        tt(R("gmk"), IND(R("hm"), R("alu")), R("gc_"), Op.mult)
+        for h in (0, 1):
+            mm(R("ps2", 16 + 8 * h, 24 + 8 * h), R("gmk", 128 * h, 128 * h + 128), R("ob8h"))
+        yield
+        ts(R("al4"), R("als"), 4.0, Op.mult, float(B0), Op.add)
+        ts(R("ahi"), R("ai"), 7, Op.arith_shift_right)
+        ts(R("alof"), R("alo"), -1.0, Op.mult)
+        tc(R("ahif"), R("ahi"))
+        yield
+        tc(R("cdi"), R("ps2", 16, 32))
+        ts(R("hh"), R("cdi"), 31, Op.bitwise_and)
+        ts(R("tl"), R("cdi"), 5, Op.arith_shift_right)
+        tt(R("xx"), R("hh"), R("ps2", 0, 16), Op.add)
+        yield
+        tt(R("blk"), R("xx"), R("tl"), Op.is_ge)
+        mm(R("ps2", 32, 40), R("tri"), R("blk", 0, 8))
+        mm(R("ps2", 40, 48), R("tri"), R("blk", 8, 16), True, False)
+        mm(R("ps2", 40, 48), R("ones"), R("blk", 0, 8), False, True)
+        ts(R("x3"), R("xx"), 3, Op.bitwise_and)
+        tt(R("d1"), R("xx"), R("tl"), Op.subtract)
+        ts(R("b4"), R("blk"), 4.0, Op.mult)
+        ts(R("s2"), R("d1"), 4.0, Op.is_lt)
+        tt(R("y1"), R("x3"), R("b4"), Op.add)
+        if t < ASKS:
+            ts(R("pv1"), R("x3"), 256.0, Op.mult)
+            tt(R("pv2"), R("pv1"), R("ps1", 272, 288), Op.add)
+        yield
+        ts(R("s1"), R("ps2", 32, 48), -384.0, Op.is_lt, 8.0, Op.mult)
+        tt(R("p8"), R("s1"), R("s2"), Op.mult)
+        tt(R("yv"), R("y1"), R("p8"), Op.add)
+        yield
+        tt(R("ay"), IND(R("yv"), R("e16")), R("mask16"), Op.mult)
+        for h in (0, 1):
+            mm(R("ps2", 48 + 8 * h, 56 + 8 * h), R("ay", 128 * h, 128 * h + 128), R("ob8"))
+        yield
+
+    def offsets(t):
+        ts(R("pp"), R("ps2", 48, 64), 4.0, Op.is_lt)
+        tt(R("oq"), R("ps2", 48, 64), R("al4"), Op.add)
+        tt(R("offu"), R("oq"), R("pp"), Op.mult)
+        yield
+        ts(R("sb"), R("ps2", 48, 64), 4.0, Op.is_ge, 2048.0, Op.mult)
+        tt(R("sou"), R("sb"), R("als"), Op.add)
+        ts(R("pt"), R("ps2", 48, 64), 8.0, Op.is_ge, 32.0, Op.mult)
+        tt(R("wl"), R("pp"), R("pt"), Op.add)
+        yield
+
+    def ask(t):
+        to = (rank + 1 + t % (N - 1)) % N
+        tc(R("ri"), R("ps2", 32, 48))
+        ts(R("pv3"), R("p8"), 262144.0, Op.mult)
+        tt(R("pv"), R("pv2"), R("pv3"), Op.add)
+        ts(R("rlo"), R("ri"), 15, Op.bitwise_and)
+        ts(R("rhi"), R("ri"), 4, Op.arith_shift_right)
+        yield
+        tt(R("cb"), IND(R("rhi"), R("e8")), R("patc8"), Op.is_equal)
+        tt(R("ca"), IND(R("rlo"), R("e16")), R("pat16"), Op.is_equal)
+        tt(R("cb2"), IND(R("pv"), R("e8")), R("cb"), Op.mult)
+        for h in (0, 1):
+            mm(R("ps5", 384, 448), R("ca", 128 * h, 128 * h + 128), R("cb2", 64 * h, 64 * h + 64), h == 0, h == 1)
+        yield
+        qp = R("qp%d" % t)
+        tt(R("cm"), R("ps5", 384, 448), R("gm"), Op.mult)
+        tt(R("c1"), R("cm", 0, 32), R("cm", 32, 64), Op.add)
+        tt(R("c2"), R("c1", 0, 16), R("c1", 16, 32), Op.add)
+        tt(qp, R("c2", 0, 8), R("c2", 8, 16), Op.add)
+        send(to, R("qpin%d" % t), qp, "rp%d" % t)
+        ts(R("lni"), qp, 255, Op.bitwise_and)
+        tc(R("lnu"), R("lni"))
+        act(R("zq%d" % t), IND(R(z[0]), R("lnu")))
+        send(to, R("zqin%d" % t), R("zq%d" % t), "rz%d" % t)
+        yield
+        ts(R("v1"), qp, 8, Op.arith_shift_right)
+        ts(R("v2"), R("v1"), 8192.0, Op.is_ge)
+        tt(R("v3"), R("v1"), R("dump2"), Op.subtract)
+        tt(R("v4"), R("v3"), R("v2"), Op.mult)
+        tt(R("offr%d" % t), R("v4"), R("dump"), Op.add)
+        yield
+
+    def pops(t):
+        if t > 0:
+            wi, of, src = R("bank"), R("offr%d" % (t - 1)), R("anin%d" % (t - 1))
+            op("v", (None, wi[1]), [src, of], lambda e: e.tensor_copy(wi[0].indirect(of[0]), src[0]))
+        tt(R("zs"), IND(R("bank", 0, BD), R("offu")), R(z[0]), Op.add)
+        ts(R(z[1]), R("zs"), 0.0, Op.max, 255.0, Op.min)
+        mm(R("ps3", 0, 256), R("ones"), R("rowc"), True, False)
+        for h in (0, 1):
+            for m in range(16):
+                mm(R("ps3", 128 * h + m, 128 * h + 128, 16), R("cc", 2048 * h + m, 2048 * h + 2048, 16), R("om16"), False, False)
+        mm(R("ps4", 0, 256), R("idb"), R(z[1]))
+        tc(R("sp"), IND(R("sui"), R("sou")))
+        for c in range(16):
+            actf(R("rd", 128 * c, 128 * c + 128), R("i128"), Fn.Abs, R("alof", c, c + 1), 1.0)
+        for c in range(0, 16, 4):
+            actf(R("rh", 128 * c, 128 * c + 512), R("rd", 128 * c, 128 * c + 512), Fn.Relu, 1.0, -1.0)
+
+    def update(t):
+        for c in range(16):
+            ts(R("lh", 128 * c, 128 * c + 128), R("rp"), R("ahif", c, c + 1), Op.is_equal, R("wl", c, c + 1), Op.mult)
+            mm(R("ps5", 128, 256), R("lh", 128 * c, 128 * c + 128), R("rh", 128 * c, 128 * c + 128), c == 0, c == 15)
+            yield
+        tt(R("cw"), R("cw"), R("ps5", 128, 256), Op.add)
+        yield
+
+    def dist(t):
+        for m in range(16):
+            tt(R("mx", 256 * m, 256 * m + 256), R("cc", m, 4096, 16), R("ps4", 0, 256), Op.max)
+            for h in (0, 1):
+                a = 256 * m + 128 * h
+                mm(R("ps3", 128 * h + m, 128 * h + 128, 16), R("mx", a, a + 128), R("o32"), False, h == 1 and m == 15)
+            yield
+
+    def choose(t):
+        tc(R("ko"), R("ps3", 1, 256, 2))
+        tt(R("k1"), R("ps3", 0, 256, 2), R("ko"), Op.min)
+        act(R("ks"), R("ps3", 0, 256))
+        yield
+        src, w = "k1", 128
+        for d in ("k2", "k3", "k4"):
+            tt(R(d), R(src, 0, w, 2), R(src, 1, w, 2), Op.min)
+            src, w = d, w // 2
+            yield
+        tt(R("oh"), IND(R("k4"), R("e16")), R("ks"), Op.is_equal)
+        for h in (0, 1):
+            mm(R("ps0", 256 + 128 * h, 384 + 128 * h), R("oh", 128 * h, 128 * h + 128), R("idb"))
+        for _ in range(4):
+            yield
+        tt(R("os"), R("ps0", 256, 512), R("sp"), Op.mult)
+        if t + 1 < STEPS:
+            for h in (0, 1):
+                mm(R("ps0", 128 * h, 128 * h + 128), R("os", 128 * h, 128 * h + 128), R("boh"))
+        spread(t + 1)
+        for _ in range(4):
+            yield
+        if t + 1 < STEPS:
+            tt(R("aa"), R("ps0", 0, 256), R("mask16"), Op.mult)
+            for h in (0, 1):
+                mm(R("ps0", 256 + 8 * h, 264 + 8 * h), R("aa", 128 * h, 128 * h + 128), R("ob8h"))
+            for _ in range(4):
+                yield
+            tc(R("als"), R("ps0", 256, 272))
+            yield
+
+    def answer(t):
+        to = (rank - 1 - t % (N - 1)) % N
+        qpin, zqin = R("qpin%d" % t), R("zqin%d" % t)
+        ts(R("qa"), qpin, 10, Op.arith_shift_right, 2047, Op.bitwise_and)
+        tc(R("qau"), R("qa"))
+        act(R("goal"), IND(R("xw"), R("qau")))
+        mm(R("ps5", 0, 128), R("bow"), zqin)
+        mm(R("ps4", 256, 384), R("idn"), zqin, True, False)
+        mm(R("ps4", 256, 384), R("idb"), R("goal"), False, True)
+        tc(R("ui"), R("ps5", 0, 128))
+        ts(R("uu"), R("ui"), 4095, Op.bitwise_and)
+        tt(R("usq"), R("uu"), R("uu"), Op.mult)
+        ts(R("um"), R("uu"), R("odd"), Op.mult)
+        ts(R("uv"), R("usq"), 5, Op.arith_shift_right)
+        tt(R("us"), R("um"), R("uv"), Op.add)
+        ts(R("ux"), R("us"), 8191, Op.bitwise_and)
+        tc(R("cou"), R("ux"))
+        for k in range(2):
+            act(R("cand", 1024 * k, 1024 * k + 1024), IND(R("bank", B0, BD), R("cou", 64 * k, 64 * k + 64)))
+        yield
+        mm(R("ps6", 0, 128), R("ones"), R("rowc", 0, 128), True, False)
+        for m in range(16):
+            mm(R("ps6", m, 128, 16), R("cand", m, 2048, 16), R("om16"), False, False)
+        for m in range(16):
+            tt(R("mq", 128 * m, 128 * m + 128), R("cand", m, 2048, 16), R("ps4", 256, 384), Op.max)
+            mm(R("ps6", m, 128, 16), R("mq", 128 * m, 128 * m + 128), R("o32"), False, m == 15)
+            yield
+        tc(R("q0"), R("ps6", 1, 128, 2))
+        tt(R("q1"), R("ps6", 0, 128, 2), R("q0"), Op.min)
+        src, w = "q1", 64
+        for d in ("q2", "q3", "q4"):
+            yield
+            tt(R(d), R(src, 0, w, 2), R(src, 1, w, 2), Op.min)
+            src, w = d, w // 2
+        yield
+        ts(R("q5"), R("q4"), 15, Op.bitwise_and)
+        yield
+        ts(R("q6"), R("q5"), R("l16"), Op.add)
+        yield
+        tt(R("aq"), IND(R("q6"), R("e16", 0, 8)), R("mask16", 0, 128), Op.mult)
+        mm(R("ps5", 448, 456), R("aq"), R("ob8h"))
+        yield
+        tc(R("seu"), R("ps5", 448, 456))
+        yield
+        tc(R("an%d" % t), IND(R("cand"), R("seu")))
+        send(to, R("anin%d" % t), R("an%d" % t), "ra%d" % t)
+        yield
+
+    def run(gen):
+        for _ in gen:
+            pass
+
+    def weave(*gens):
+        gens = list(gens)
+        while gens:
+            for x in list(gens):
+                if x in gens and next(x, "end") == "end":
+                    gens = [y for y in gens if y is not x]
+
+    nothing = iter(())
+    run(head(0))
+    for t in range(STEPS):
+        asks, more = t < ASKS, t + 1 < STEPS
+        weave(offsets(t), ask(t) if asks else nothing)
+        pops(t)
+        run(dist(t))
+        upd, ch, ans = update(t), choose(t), answer(t) if asks else nothing
+        next(ch)
+        next(ans, 0)
+        weave(ch, upd)
+        nxt = head(t + 1) if more else nothing
+        next(nxt, 0)
+        weave(ans, nxt, ans)
+        z.reverse()
+
+    outs = [0]
+
+    def store(dst, ap, ref):
+        access("d", ref[1], [])
+        g.sync.dma_start(dst, ap).then_inc(T.sem["sout"], 16)
+        outs[0] += 16
+
+    act(R("arf"), R("ps1", 0, 256))
+    ts(R("w1"), R("cw"), 1.0, Op.mult)
+    ts(R("w2"), R("w1"), 31, Op.bitwise_and)
+    ts(R("w3"), R("w1"), 5, Op.arith_shift_right)
+    ts(R("w4"), R("w1"), 3, Op.bitwise_and)
+    tc(R("ohf"), R("w4"))
+    tt(R("oyf"), R("w3"), R("w2"), Op.subtract)
+    store(T.yz[:, :], R(z[0])[0], R(z[0]))
+    buf, base, w = PACK["arf"]
+    store(T.ya[:, :], T[buf][0:128:16, base:base + w], R("arf"))
+    store(T.yh[:, :], R("ohf")[0], R("ohf"))
+    store(T.yf[:, :], R("oyf")[0], R("oyf"))
+    g.sync.wait_ge(T.sem["sout"], outs[0])
+    for q in "vstg":
+        need("g", qsem[q], count[q], {})
+    for s in LOADS:
+        need("g", s, 16, {})
+    for s in sorted(arrive):
+        need("g", s, arrive[s], {})
+    g.wait_ge(T.sem["sent"], sends[0])

@@ -2,26 +2,28 @@ from concourse.mybir import AluOpType as Op, ActivationFunctionType as Fn
 
 STEPS = 4
 ASKS = STEPS - 1
-B0, BD, BE = 16, 8208, 8336
+NS = 4
+SBANK = ["ps6", "ps7", "ps0", "ps1"]
+B0, BD = 144, 8336
 PSUM = ["ps%d" % i for i in range(8)]
 SCRATCH = {}
 for _n in PSUM:
     SCRATCH[_n] = ("psum", [128, 512], "float32")
-WIDE = {"xw": (2048, "bfloat16"), "sui": (4096, "int32"), "bank": (BE, "bfloat16"), "hm": (2048, "bfloat16"), "cc": (4096, "bfloat16"),
+WIDE = {"xw": (2048, "bfloat16"), "sui": (4096, "int32"), "bank": (BD, "bfloat16"), "hm": (2048, "bfloat16"), "cc": (4096, "bfloat16"),
         "mx": (4096, "bfloat16"), "cand": (2048, "bfloat16"), "mq": (2048, "bfloat16"), "eb": (4096, "bfloat16"), "lh": (2048, "bfloat16"),
         "rh": (2048, "bfloat16"), "rd": (2048, "bfloat16"), "za": (256, "bfloat16"), "zb": (256, "bfloat16")}
 for _n, (_w, _d) in WIDE.items():
     SCRATCH[_n] = ("sbuf", [128, _w], _d)
 NARROW = {
-    "float32": "pcol 1 p16 1 pdiv 1 odd 1 l16 1 ge8 1 is0 1 jf 256 pat16 256 patc8 128 mask16 256 qd16 128 gm 64 rpt 128 cw 128 cwt 128 e8f 8 dump 8 dump2 8 "
-               "als 16 al4 16 alof 16 ahif 16 arm 256 gc_ 256 b4 16 d1 16 s1 16 s2 16 y1 16 p8 16 yv 16 oq 16 pp 16 sb 16 pt 16 wl 16 ks 256 ko 128 k1 128 "
-               "k2 64 k3 32 k4 16 arf 256 pv1 16 pv2 16 pv3 16 pv 16 ca 256 cb 128 cb2 128 cm 64 c1 32 c2 16 v2 8 v3 8 v4 8 um 128 q0 64 q1 64 q2 32 q3 16 "
+    "float32": "pcol 1 p16 1 pdiv 1 odd 1 l16 1 ge8 1 is0 1 jf 256 pat16 256 patc8 128 mask16 256 qd16 128 gm 64 rpt 128 cw 128 cwt 128 e8f 8 dump 8 "
+               "als 16 al4 16 alof 16 ahif 16 arm 256 gc_ 256 d1 16 s1 16 s2 16 y1 16 p8 16 yv 16 oq 16 pp 16 sb 16 pt 16 wl 16 ks 256 ko 128 k1 128 "
+               "k2 64 k3 32 k4 16 arf 256 pv1 16 pv2 16 pv3 16 pv 16 ca 256 cb 128 cb2 128 cm 64 c1 32 c2 16 v2 8 um 128 q0 64 q1 64 q2 32 q3 16 "
                "q6 8 ohf 128 oyf 128",
     "int32": "ci 1 ci2 1 ci3 1 ji 256 jt 256 hi0 128 fi0 128 a0i 16 ai 16 alo 16 ahi 16 cdi 16 hh 16 tl 16 xx 16 x3 16 ri 16 rlo 16 rhi 16 lni 8 v1 8 qa 8 "
              "ui 128 uu 128 usq 128 uv 128 us 128 ux 128 q4 8 q5 8 w1 128 w2 128 w3 128 w4 128",
     "uint16": "e16 16 e8 8 alu 16 alou 16 suu 256 offu 16 sou 16 lnu 8 qau 8 cou 128 seu 8",
-    "bfloat16": "bo 128 bow 128 ob8 8 o32 8 om16 8 idb 128 idn 128 tri 128 ones 128 rp 128 i128 128 maskm 256 lanb 16 rowc 256 dg 256 blk 16 ay 256 "
-                "zs 256 oh 256 goal 128",
+    "bfloat16": "bo 128 bow 128 ob8 8 o16 8 o32 8 om16 8 idb 128 idn 128 tri 128 ones 128 quar 128 rp 128 i128 128 maskm 256 lanb 16 rowc 256 zer 16 dg 256 "
+                "blk 16 ay 256 zs 256 oh 256 goal 128",
     "float16": "boh 128 ob8h 8 ob8k 8 arow 256 os 256 gmk 256 sp 256 aa 256 aq 128"}
 PACK = {}
 for _d, _t in NARROW.items():
@@ -135,8 +137,8 @@ def rank_program(g, core, T, topo):
         for name, lo, hi in ref[1]:
             recs.setdefault(name, []).append((lo, hi, True, q, sem, n, {}))
 
-    def load(out, src, sem):
-        g.sync.dma_start(out[0], src).then_inc(T.sem[sem], 16)
+    def load(q, out, src, sem):
+        qobj[q].dma_start(out[0], src).then_inc(T.sem[sem], 16)
         landed(out, "dma", sem, 16)
 
     sends = [0]
@@ -148,13 +150,13 @@ def rank_program(g, core, T, topo):
         g.remote_dma(out[0], src[0], T.sem[sem], T.sem["sent"], pid, rid, topo.mask(core, dst))
         sends[0] += len(topo.engines(core, dst))
 
-    load(R("a0i"), T.a0[:, :], "la")
-    load(R("hi0"), T.hd0[:, :], "lh0")
-    load(R("fi0"), T.fl0[:, :], "lf0")
-    load(R("sui", 0, 2048), T.su[:, :], "ls")
-    load(R("xw"), T.xs[:, :], "lx")
-    load(R("za"), T.z0[:, :], "lz")
-    load(R("bank", B0, BD), T.gs[:, :], "lg")
+    load("d", R("a0i"), T.a0[:, :], "la")
+    load("s", R("hi0"), T.hd0[:, :], "lh0")
+    load("s", R("fi0"), T.fl0[:, :], "lf0")
+    load("d", R("sui", 0, 2048), T.su[:, :], "ls")
+    load("s", R("za"), T.z0[:, :], "lz")
+    load("d", R("xw"), T.xs[:, :], "lx")
+    load("d", R("bank", B0, BD), T.gs[:, :], "lg")
     arrive = {}
     for t in range(ASKS):
         asker, asked = T.cores[(rank - 1 - t % (N - 1)) % N], T.cores[(rank + 1 + t % (N - 1)) % N]
@@ -181,12 +183,12 @@ def rank_program(g, core, T, topo):
     ts(R("ob8h"), R("jf", 0, 8), R("pdiv"), Op.is_equal)
     ts(R("ob8k"), R("ob8h"), 1024.0, Op.mult)
     ts(R("maskm"), R("pat16"), R("p16"), Op.is_le, 4096.0, Op.mult)
-    ts(R("bo"), R("qd16"), R("pdiv"), Op.is_equal)
     ts(R("ob8"), R("jf", 0, 8), R("pdiv"), Op.is_equal)
     ts(R("idb"), R("jf", 0, 128), R("pcol"), Op.is_equal)
     ts(R("lanb", 0, 8), R("jf", 0, 8), 0.0, Op.mult, R("pcol"), Op.add)
     ts(R("lanb", 8, 16), R("lanb", 0, 8), 128.0, Op.add)
     fill(R("ones"), 1.0)
+    fill(R("zer"), 0.0)
     for j in range(16):
         actf(R("hm", 128 * j, 128 * j + 128), R("ones"), Fn.Copy, 0.0, R("mask16", j, j + 1))
     tc(R("als"), R("a0i"))
@@ -205,21 +207,16 @@ def rank_program(g, core, T, topo):
                 mm(o, R("idb"), R("lanb", 8 * h, 8 * h + 8), False, True)
 
     spread(0)
-    fill(R("eb"), 0.0)
+    for c in range(15):
+        if c != 7:
+            fill(R("eb", 256 * c + 128 * (c >= 8), 272 * c + 16), 0.0)
     fill(R("bank", 0, B0), 0.0)
-    ts(R("idn"), R("idb"), -1.0, Op.mult)
+    ts(R("bo"), R("qd16"), R("pdiv"), Op.is_equal)
     ts(R("rpt"), R("idb"), 512.0, Op.mult)
     ts(R("cwt"), R("jf", 0, 128), R("pcol"), Op.is_gt)
-    tt(R("tri"), R("cwt"), R("rpt"), Op.subtract)
-    ts(R("i128"), R("jf", 0, 128), 0.0, Op.add)
-    ts(R("rpt"), R("pat16", 0, 128), 1.0, Op.add)
-    tt(R("rpt"), R("rpt"), R("bo"), Op.mult)
-    ts(R("rp"), R("rpt"), -1.0, Op.add)
-    ts(R("o32"), R("ob8"), 32.0, Op.mult)
-    ts(R("om16"), R("ob8"), -16.0, Op.mult)
-    ts(R("odd"), R("p16"), 2.0, Op.mult, 1.0, Op.add)
-    ts(R("bow"), R("bo"), R("odd"), Op.mult)
-    ts(R("l16"), R("pcol"), 16.0, Op.mult)
+    tt(R("cwt"), R("cwt"), R("rpt"), Op.subtract)
+    ts(R("tri"), R("cwt"), 0.25, Op.mult)
+    fill(R("quar"), 0.25)
     ts(R("ge8"), R("p16"), 8.0, Op.is_ge)
     ts(R("e8f"), R("jf", 0, 8), 2.0, Op.mult, R("ge8"), Op.add)
     tc(R("e8"), R("e8f"))
@@ -227,64 +224,90 @@ def rank_program(g, core, T, topo):
     ts(R("patc8"), R("jt", 0, 128), -32.0, Op.add)
     ts(R("jt", 0, 64), R("ji", 0, 64), 3, Op.arith_shift_right)
     ts(R("gm"), R("jt", 0, 64), R("pdiv"), Op.is_equal)
-    ts(R("dump"), R("jf", 0, 8), 16.0, Op.mult, R("p16"), Op.add)
-    ts(R("dump2"), R("dump"), float(BD + 8192 - B0), Op.add)
-    ts(R("dump"), R("dump"), float(BD), Op.add)
-    ts(R("is0"), R("pcol"), 0.0, Op.is_equal)
-    ts(R("rowc"), R("pat16"), R("is0"), Op.mult)
     ts(R("cwt"), R("hi0"), 33.0, Op.mult)
     ts(R("cw"), R("fi0"), 32.0, Op.mult)
     tt(R("cw"), R("cw"), R("cwt"), Op.add)
 
+    def late_constants():
+        ts(R("dump"), R("jf", 0, 8), 16.0, Op.mult, R("p16"), Op.add)
+        ts(R("dump"), R("dump"), float(16 + 16384 - B0), Op.add)
+        ts(R("is0"), R("pcol"), 0.0, Op.is_equal)
+        ts(R("rowc"), R("pat16"), R("is0"), Op.mult)
+        ts(R("om16"), R("ob8"), -16.0, Op.mult)
+        ts(R("idn"), R("idb"), -1.0, Op.mult)
+        ts(R("o16"), R("ob8"), 16.0, Op.mult)
+        ts(R("o32"), R("ob8"), 32.0, Op.mult)
+        ts(R("i128"), R("jf", 0, 128), 0.0, Op.add)
+        ts(R("rpt"), R("pat16", 0, 128), 1.0, Op.add)
+        tt(R("rpt"), R("rpt"), R("bo"), Op.mult)
+        ts(R("rp"), R("rpt"), -1.0, Op.add)
+        ts(R("odd"), R("p16"), 2.0, Op.mult, 1.0, Op.add)
+        ts(R("bow"), R("bo"), R("odd"), Op.mult)
+        ts(R("l16"), R("pcol"), 16.0, Op.mult)
+
     z = ["za", "zb"]
+
+    def centres(a, b):
+        for k in range(a, b):
+            act(R("cc", 1024 * k, 1024 * k + 1024), IND(R("xw"), R("suu", 64 * k, 64 * k + 64)))
+
+    def differences():
+        for c in range(16):
+            actf(R("rd", 128 * c, 128 * c + 128), R("i128"), Fn.Abs, R("alof", c, c + 1), 1.0)
 
     def head(t):
         tc(R("ai"), R("als"))
         tc(R("alu"), R("als"))
         ts(R("alo"), R("ai"), 127, Op.bitwise_and)
-        tc(R("suu"), IND(R("sui", 0, 2048), R("alu")))
+        if t > 0:
+            tc(R("suu"), IND(R("sui", 0, 2048), R("alu")))
         tc(R("alou"), R("alo"))
         if t > 0:
-            act(R("gc_"), IND(R("cw"), R("alou")))
-        for k in range(4):
-            act(R("cc", 1024 * k, 1024 * k + 1024), IND(R("xw"), R("suu", 64 * k, 64 * k + 64)))
-            if t == 0 and k == 1:
-                act(R("gc_"), IND(R("cw"), R("alou")))
-        yield
+            centres(0, 2)
         tc(R("arow"), R("ps1", 0, 256))
+        mm(R("ps2", 0, 16), R("ones"), R("zer"), True, False)
+        yield
+        act(R("gc_"), IND(R("cw"), R("alou")))
+        if t > 0:
+            centres(2, 4)
         yield
         for c in range(15):
             ts(R("eb", 272 * c + 16, 256 * c + 256), R("arow", 16 * c + 16, 256), R("als", c, c + 1), Op.is_equal)
+            for h in (0, 1) if c < 7 else (1,):
+                mm(R("ps2", 8 * h, 8 * h + 8), R("eb", 256 * c + 128 * h, 256 * c + 128 * h + 128), R("ob8"), False, c == 14)
             yield
-        tt(R("dg"), IND(R("als"), R("e16")), R("arm"), Op.is_equal)
-        for h in (0, 1):
-            for c in range(7 if h == 0 else 15):
-                mm(R("ps2", 8 * h, 8 * h + 8), R("eb", 256 * c + 128 * h, 256 * c + 128 * h + 128), R("ob8"), c == 0, False)
-            mm(R("ps2", 8 * h, 8 * h + 8), R("dg", 128 * h, 128 * h + 128), R("ob8"), False, True)
-        yield
+            if c == 6:
+                tt(R("dg"), IND(R("als"), R("e16")), R("arm"), Op.is_equal)
+                for h in (0, 1):
+                    mm(R("ps2", 8 * h, 8 * h + 8), R("dg", 128 * h, 128 * h + 128), R("ob8"), False, False)
+                yield
+        if t == 0:
+            tc(R("suu"), IND(R("sui", 0, 2048), R("alu")))
+            centres(0, 4)
         tt(R("gmk"), IND(R("hm"), R("alu")), R("gc_"), Op.mult)
         for h in (0, 1):
-            mm(R("ps2", 16 + 8 * h, 24 + 8 * h), R("gmk", 128 * h, 128 * h + 128), R("ob8h"))
+            mm(R("ps7", 8 * h, 8 * h + 8), R("gmk", 128 * h, 128 * h + 128), R("ob8h"))
         yield
         ts(R("al4"), R("als"), 4.0, Op.mult, float(B0), Op.add)
         ts(R("ahi"), R("ai"), 7, Op.arith_shift_right)
-        ts(R("alof"), R("alo"), -1.0, Op.mult)
-        tc(R("ahif"), R("ahi"))
         yield
-        tc(R("cdi"), R("ps2", 16, 32))
+        tc(R("cdi"), R("ps7", 0, 16))
+        ts(R("alof"), R("alo"), -1.0, Op.mult)
         ts(R("hh"), R("cdi"), 31, Op.bitwise_and)
         ts(R("tl"), R("cdi"), 5, Op.arith_shift_right)
         tt(R("xx"), R("hh"), R("ps2", 0, 16), Op.add)
+        tc(R("ahif"), R("ahi"))
+        if t > 0:
+            differences()
         yield
-        tt(R("blk"), R("xx"), R("tl"), Op.is_ge)
+        tt(R("d1"), R("xx"), R("tl"), Op.subtract)
+        ts(R("x3"), R("xx"), 3, Op.bitwise_and)
+        ts(R("blk"), R("d1"), 0.0, Op.is_ge, 4.0, Op.mult)
         mm(R("ps2", 32, 40), R("tri"), R("blk", 0, 8))
         mm(R("ps2", 40, 48), R("tri"), R("blk", 8, 16), True, False)
-        mm(R("ps2", 40, 48), R("ones"), R("blk", 0, 8), False, True)
-        ts(R("x3"), R("xx"), 3, Op.bitwise_and)
-        tt(R("d1"), R("xx"), R("tl"), Op.subtract)
-        ts(R("b4"), R("blk"), 4.0, Op.mult)
+        mm(R("ps2", 40, 48), R("quar"), R("blk", 0, 8), False, True)
         ts(R("s2"), R("d1"), 4.0, Op.is_lt)
-        tt(R("y1"), R("x3"), R("b4"), Op.add)
+        tt(R("y1"), R("x3"), R("blk"), Op.add)
         if t < ASKS:
             ts(R("pv1"), R("x3"), 256.0, Op.mult)
             tt(R("pv2"), R("pv1"), R("ps1", 272, 288), Op.add)
@@ -309,10 +332,22 @@ def rank_program(g, core, T, topo):
         tt(R("wl"), R("pp"), R("pt"), Op.add)
         yield
 
+    made = [0]
+
+    def onehot(c):
+        if c >= made[0]:
+            made[0] = c + 1
+            ts(R("lh", 128 * c, 128 * c + 128), R("rp"), R("ahif", c, c + 1), Op.is_equal, R("wl", c, c + 1), Op.mult)
+
+    def onehots(n):
+        for _ in range(n):
+            if made[0] < 16:
+                onehot(made[0])
+
     def ask(t):
         to = (rank + 1 + t % (N - 1)) % N
         tc(R("ri"), R("ps2", 32, 48))
-        ts(R("pv3"), R("p8"), 262144.0, Op.mult)
+        ts(R("pv3"), R("p8"), 524288.0, Op.mult)
         tt(R("pv"), R("pv2"), R("pv3"), Op.add)
         ts(R("rlo"), R("ri"), 15, Op.bitwise_and)
         ts(R("rhi"), R("ri"), 4, Op.arith_shift_right)
@@ -323,6 +358,10 @@ def rank_program(g, core, T, topo):
         for h in (0, 1):
             mm(R("ps5", 384, 448), R("ca", 128 * h, 128 * h + 128), R("cb2", 64 * h, 64 * h + 64), h == 0, h == 1)
         yield
+        if t == 0:
+            late_constants()
+        else:
+            onehots(8)
         qp = R("qp%d" % t)
         tt(R("cm"), R("ps5", 384, 448), R("gm"), Op.mult)
         tt(R("c1"), R("cm", 0, 32), R("cm", 32, 64), Op.add)
@@ -335,44 +374,56 @@ def rank_program(g, core, T, topo):
         send(to, R("zqin%d" % t), R("zq%d" % t), "rz%d" % t)
         yield
         ts(R("v1"), qp, 8, Op.arith_shift_right)
-        ts(R("v2"), R("v1"), 8192.0, Op.is_ge)
-        tt(R("v3"), R("v1"), R("dump2"), Op.subtract)
-        tt(R("v4"), R("v3"), R("v2"), Op.mult)
-        tt(R("offr%d" % t), R("v4"), R("dump"), Op.add)
+        tt(R("v2"), R("v1"), R("dump"), Op.max)
+        ts(R("offr%d" % t), R("v2"), float(B0 - 16384), Op.add)
         yield
 
     def pops(t):
         if t > 0:
             wi, of, src = R("bank"), R("offr%d" % (t - 1)), R("anin%d" % (t - 1))
             op("v", (None, wi[1]), [src, of], lambda e: e.tensor_copy(wi[0].indirect(of[0]), src[0]))
-        tt(R("zs"), IND(R("bank", 0, BD), R("offu")), R(z[0]), Op.add)
+        tt(R("zs"), IND(R("bank"), R("offu")), R(z[0]), Op.add)
         ts(R(z[1]), R("zs"), 0.0, Op.max, 255.0, Op.min)
         mm(R("ps3", 0, 256), R("ones"), R("rowc"), True, False)
         for h in (0, 1):
-            for m in range(16):
+            for m in range(16 - NS):
                 mm(R("ps3", 128 * h + m, 128 * h + 128, 16), R("cc", 2048 * h + m, 2048 * h + 2048, 16), R("om16"), False, False)
+        for m in range(16 - NS, 16):
+            mm(R(SBANK[m % NS], 0, 256), R("idb"), R("cc", m, 4096, 16), True, False)
         mm(R("ps4", 0, 256), R("idb"), R(z[1]))
+        for m in range(16 - NS, 16):
+            mm(R(SBANK[m % NS], 0, 256), R("idn"), R(z[1]), False, True)
+            actf(R("mx", 256 * m, 256 * m + 256), R(SBANK[m % NS], 0, 256), Fn.Abs, 0.0, 1.0)
         tc(R("sp"), IND(R("sui"), R("sou")))
-        for c in range(16):
-            actf(R("rd", 128 * c, 128 * c + 128), R("i128"), Fn.Abs, R("alof", c, c + 1), 1.0)
+        if t == 0:
+            differences()
         for c in range(0, 16, 4):
             actf(R("rh", 128 * c, 128 * c + 512), R("rd", 128 * c, 128 * c + 512), Fn.Relu, 1.0, -1.0)
 
     def update(t):
         for c in range(16):
-            ts(R("lh", 128 * c, 128 * c + 128), R("rp"), R("ahif", c, c + 1), Op.is_equal, R("wl", c, c + 1), Op.mult)
+            onehot(c)
             mm(R("ps5", 128, 256), R("lh", 128 * c, 128 * c + 128), R("rh", 128 * c, 128 * c + 128), c == 0, c == 15)
             yield
+
+    def table():
         tt(R("cw"), R("cw"), R("ps5", 128, 256), Op.add)
-        yield
 
     def dist(t):
-        for m in range(16):
+        for m in range(16 - NS):
             tt(R("mx", 256 * m, 256 * m + 256), R("cc", m, 4096, 16), R("ps4", 0, 256), Op.max)
             for h in (0, 1):
                 a = 256 * m + 128 * h
-                mm(R("ps3", 128 * h + m, 128 * h + 128, 16), R("mx", a, a + 128), R("o32"), False, h == 1 and m == 15)
-            yield
+                mm(R("ps3", 128 * h + m, 128 * h + 128, 16), R("mx", a, a + 128), R("o32"), False, False)
+            if m == 3:
+                for n in range(16 - NS, 16):
+                    for h in (0, 1):
+                        mm(R("ps3", 128 * h + n, 128 * h + 128, 16), R(z[1], 128 * h, 128 * h + 128), R("o16"), False, False)
+            if m == 15 - NS:
+                for n in range(16 - NS, 16):
+                    for h in (0, 1):
+                        a = 256 * n + 128 * h
+                        mm(R("ps3", 128 * h + n, 128 * h + 128, 16), R("mx", a, a + 128), R("o16"), False, h == 1 and n == 15)
 
     def choose(t):
         tc(R("ko"), R("ps3", 1, 256, 2))
@@ -393,17 +444,19 @@ def rank_program(g, core, T, topo):
         if t + 1 < STEPS:
             for h in (0, 1):
                 mm(R("ps0", 128 * h, 128 * h + 128), R("os", 128 * h, 128 * h + 128), R("boh"))
+            for _ in range(4):
+                yield
+            tt(R("aa"), R("ps0", 0, 256), R("mask16"), Op.mult)
+            for h in (0, 1):
+                mm(R("ps0", 256 + 8 * h, 264 + 8 * h), R("aa", 128 * h, 128 * h + 128), R("ob8h"))
         spread(t + 1)
         for _ in range(4):
             yield
         if t + 1 < STEPS:
-            tt(R("aa"), R("ps0", 0, 256), R("mask16"), Op.mult)
-            for h in (0, 1):
-                mm(R("ps0", 256 + 8 * h, 264 + 8 * h), R("aa", 128 * h, 128 * h + 128), R("ob8h"))
-            for _ in range(4):
-                yield
             tc(R("als"), R("ps0", 256, 272))
-            yield
+        else:
+            act(R("arf"), R("ps1", 0, 256))
+        yield
 
     def answer(t):
         to = (rank - 1 - t % (N - 1)) % N
@@ -415,16 +468,22 @@ def rank_program(g, core, T, topo):
         mm(R("ps4", 256, 384), R("idn"), zqin, True, False)
         mm(R("ps4", 256, 384), R("idb"), R("goal"), False, True)
         tc(R("ui"), R("ps5", 0, 128))
+        yield
         ts(R("uu"), R("ui"), 4095, Op.bitwise_and)
+        yield
         tt(R("usq"), R("uu"), R("uu"), Op.mult)
         ts(R("um"), R("uu"), R("odd"), Op.mult)
+        yield
         ts(R("uv"), R("usq"), 5, Op.arith_shift_right)
+        yield
         tt(R("us"), R("um"), R("uv"), Op.add)
+        yield
         ts(R("ux"), R("us"), 8191, Op.bitwise_and)
+        yield
         tc(R("cou"), R("ux"))
         for k in range(2):
             act(R("cand", 1024 * k, 1024 * k + 1024), IND(R("bank", B0, BD), R("cou", 64 * k, 64 * k + 64)))
-        yield
+        yield "gathering"
         mm(R("ps6", 0, 128), R("ones"), R("rowc", 0, 128), True, False)
         for m in range(16):
             mm(R("ps6", m, 128, 16), R("cand", m, 2048, 16), R("om16"), False, False)
@@ -453,9 +512,31 @@ def rank_program(g, core, T, topo):
         send(to, R("anin%d" % t), R("an%d" % t), "ra%d" % t)
         yield
 
+    def finish(t):
+        for _ in update(t):
+            yield
+        for _ in range(3):
+            yield
+        table()
+        ts(R("w1"), R("cw"), 1.0, Op.mult)
+        yield
+        ts(R("w2"), R("w1"), 31, Op.bitwise_and)
+        ts(R("w3"), R("w1"), 5, Op.arith_shift_right)
+        ts(R("w4"), R("w1"), 3, Op.bitwise_and)
+        yield
+        tt(R("oyf"), R("w3"), R("w2"), Op.subtract)
+        tc(R("ohf"), R("w4"))
+        yield
+
     def run(gen):
         for _ in gen:
             pass
+
+    def until(x, tag):
+        for y in x:
+            yield
+            if y == tag:
+                return
 
     def weave(*gens):
         gens = list(gens)
@@ -470,14 +551,21 @@ def rank_program(g, core, T, topo):
         asks, more = t < ASKS, t + 1 < STEPS
         weave(offsets(t), ask(t) if asks else nothing)
         pops(t)
-        run(dist(t))
-        upd, ch, ans = update(t), choose(t), answer(t) if asks else nothing
+        dist(t)
+        ch, ans = choose(t), answer(t) if asks else nothing
+        onehots(4)
         next(ch)
-        next(ans, 0)
-        weave(ch, upd)
-        nxt = head(t + 1) if more else nothing
-        next(nxt, 0)
-        weave(ans, nxt, ans)
+        if more:
+            weave(until(ans, "gathering"), ch, update(t))
+            nxt = head(t + 1)
+            next(nxt)
+            table()
+            for _ in range(5):
+                next(nxt)
+            weave(ans, nxt, ans)
+        else:
+            weave(finish(t), ch)
+        made[0] = 0
         z.reverse()
 
     outs = [0]
@@ -487,18 +575,11 @@ def rank_program(g, core, T, topo):
         g.sync.dma_start(dst, ap).then_inc(T.sem["sout"], 16)
         outs[0] += 16
 
-    act(R("arf"), R("ps1", 0, 256))
-    ts(R("w1"), R("cw"), 1.0, Op.mult)
-    ts(R("w2"), R("w1"), 31, Op.bitwise_and)
-    ts(R("w3"), R("w1"), 5, Op.arith_shift_right)
-    ts(R("w4"), R("w1"), 3, Op.bitwise_and)
-    tc(R("ohf"), R("w4"))
-    tt(R("oyf"), R("w3"), R("w2"), Op.subtract)
     store(T.yz[:, :], R(z[0])[0], R(z[0]))
     buf, base, w = PACK["arf"]
     store(T.ya[:, :], T[buf][0:128:16, base:base + w], R("arf"))
-    store(T.yh[:, :], R("ohf")[0], R("ohf"))
     store(T.yf[:, :], R("oyf")[0], R("oyf"))
+    store(T.yh[:, :], R("ohf")[0], R("ohf"))
     g.sync.wait_ge(T.sem["sout"], outs[0])
     for q in "vstg":
         need("g", qsem[q], count[q], {})

from concourse.mybir import AluOpType as Op, ActivationFunctionType as Fn

STEPS = 4
ASKS = STEPS - 1
NS = 4
SBANK = ["ps6", "ps7", "ps0", "ps1"]
B0, BD = 144, 8336
PSUM = ["ps%d" % i for i in range(8)]
SCRATCH = {}
for _n in PSUM:
    SCRATCH[_n] = ("psum", [128, 512], "float32")
WIDE = {"xw": (2048, "bfloat16"), "sui": (4096, "int32"), "bank": (BD, "bfloat16"), "hm": (2048, "bfloat16"), "cc": (4096, "bfloat16"),
        "mx": (4096, "bfloat16"), "cand": (2048, "bfloat16"), "mq": (2048, "bfloat16"), "eb": (4096, "bfloat16"), "lh": (2048, "bfloat16"),
        "rh": (2048, "bfloat16"), "rd": (2048, "bfloat16"), "za": (256, "bfloat16"), "zb": (256, "bfloat16")}
for _n, (_w, _d) in WIDE.items():
    SCRATCH[_n] = ("sbuf", [128, _w], _d)
NARROW = {
    "float32": "pcol 1 p16 1 pdiv 1 odd 1 l16 1 ge8 1 is0 1 jf 256 pat16 256 patc8 128 mask16 256 qd16 128 gm 64 rpt 128 cw 128 cwt 128 e8f 8 dump 8 "
               "als 16 al4 16 alof 16 ahif 16 arm 256 gc_ 256 d1 16 s1 16 s2 16 y1 16 p8 16 yv 16 oq 16 pp 16 sb 16 pt 16 wl 16 ks 256 ko 128 k1 128 "
               "k2 64 k3 32 k4 16 arf 256 pv1 16 pv2 16 pv3 16 pv 16 ca 256 cb 128 cb2 128 cm 64 c1 32 c2 16 v2 8 um 128 q0 64 q1 64 q2 32 q3 16 "
               "q6 8 ohf 128 oyf 128",
    "int32": "ci 1 ci2 1 ci3 1 ji 256 jt 256 hi0 128 fi0 128 a0i 16 ai 16 alo 16 ahi 16 cdi 16 hh 16 tl 16 xx 16 x3 16 ri 16 rlo 16 rhi 16 lni 8 v1 8 qa 8 "
             "ui 128 uu 128 usq 128 uv 128 us 128 ux 128 q4 8 q5 8 w1 128 w2 128 w3 128 w4 128",
    "uint16": "e16 16 e8 8 alu 16 alou 16 suu 256 offu 16 sou 16 lnu 8 qau 8 cou 128 seu 8",
    "bfloat16": "bo 128 bow 128 ob8 8 o16 8 o32 8 om16 8 idb 128 idn 128 tri 128 ones 128 quar 128 rp 128 i128 128 maskm 256 lanb 16 rowc 256 zer 16 dg 256 "
                "blk 16 ay 256 zs 256 oh 256 goal 128",
    "float16": "boh 128 ob8h 8 ob8k 8 arow 256 os 256 gmk 256 sp 256 aa 256 aq 128"}
PACK = {}
for _d, _t in NARROW.items():
    _at, _f = 0, _t.split()
    for _n, _w in zip(_f[::2], _f[1::2]):
        PACK[_n] = ("pk_" + _d, _at, int(_w))
        _at += -(-int(_w) // 16) * 16
    SCRATCH["pk_" + _d] = ("sbuf", [128, _at], _d)
for _t in range(ASKS):
    for _n, _w, _d in (("qp", 8, "int32"), ("zq", 128, "bfloat16"), ("an", 128, "bfloat16"),
                       ("qpin", 8, "int32"), ("zqin", 128, "bfloat16"), ("anin", 128, "bfloat16"), ("offr", 8, "uint16")):
        SCRATCH["%s%d" % (_n, _t)] = ("sbuf", [128, _w], _d)
LOADS = ["la", "ls", "lx", "lh0", "lf0", "lz", "lg"]
SEMAPHORES = ["sv", "ss", "st", "sg", "sent", "sout"] + LOADS + ["%s%d" % (n, t) for t in range(ASKS) for n in ("rp", "rz", "ra")]


def rank_program(g, core, T, topo):
    rank = T.rank_of(core)
    if rank is None:
        return
    N = len(T.cores)
    qobj = {"v": g.vector, "s": g.scalar, "t": g.tensor, "g": g, "d": g.sync}
    qsem = {"v": "sv", "s": "ss", "t": "st", "g": "sg"}
    count = {"v": 0, "s": 0, "t": 0, "g": 0}
    known = {q: {} for q in qobj}
    recs = {}

    def need(q, sem, n, snap):
        kn = known[q]
        if kn.get(sem, 0) < n:
            qobj[q].wait_ge(T.sem[sem], n)
            kn[sem] = n
            for a, b in snap.items():
                if kn.get(a, 0) < b:
                    kn[a] = b

    def access(q, reads, writes):
        todo = {}
        for wr, refs in ((False, reads), (True, writes)):
            for name, lo, hi in refs:
                for r in recs.get(name, ()):
                    hit = r[3] != q if name in PSUM else r[0] < hi and lo < r[1] and (r[2] or wr)
                    if hit and (r[4] not in todo or todo[r[4]][0] < r[5]):
                        todo[r[4]] = (r[5], r[6])
        for sem in sorted(todo, key=lambda s: -len(todo[s][1])):
            need(q, sem, todo[sem][0], todo[sem][1])

    def note(q, sem, n, reads, writes):
        snap = dict(known[q])
        for wr, refs in ((False, reads), (True, writes)):
            for name, lo, hi in refs:
                old = recs.get(name, [])
                if name in PSUM:
                    old = [r for r in old if r[3] != q]
                elif wr:
                    old = [r for r in old if not (lo <= r[0] and r[1] <= hi)]
                else:
                    old = [r for r in old if r[2] or r[3] != q or not (lo <= r[0] and r[1] <= hi)]
                old.append((lo, hi, wr, q, sem, n, snap))
                recs[name] = old

    def op(q, out, ins, emit):
        reads = [x for r in ins for x in r[1]]
        access(q, reads, out[1])
        count[q] += 1
        emit(qobj[q]).then_inc(T.sem[qsem[q]], 1)
        note(q, qsem[q], count[q], reads, out[1])

    def R(name, a=0, b=None, st=1):
        buf, base, w = PACK[name] if name in PACK else (name, 0, SCRATCH[name][1][1])
        b = w if b is None else b
        ap = T[buf][:, base + a:base + b] if st == 1 else T[buf][:, base + a:base + b:st]
        return (ap, [(buf, base + a, base + b)])

    def IND(win, off):
        return (win[0].indirect(off[0]), win[1] + off[1])

    def sc(x):
        return x[0] if isinstance(x, tuple) else x

    def tc(out, a):
        op("v", out, [a], lambda e: e.tensor_copy(out[0], a[0]))

    def tt(out, a, b, o):
        op("v", out, [a, b], lambda e: e.tensor_tensor(out[0], a[0], b[0], o))

    def ts(out, a, s1, o1, s2=None, o2=None):
        ins = [a] + [s for s in (s1, s2) if isinstance(s, tuple)]
        if o2 is None:
            op("v", out, ins, lambda e: e.tensor_scalar(out[0], a[0], sc(s1), None, o1))
        else:
            op("v", out, ins, lambda e: e.tensor_scalar(out[0], a[0], sc(s1), sc(s2), o1, o2))

    def act(out, a):
        op("s", out, [a], lambda e: e.activation(out[0], a[0], Fn.Copy))

    def actf(out, a, fn, bias, scale):
        ins = [a] + [s for s in (bias, scale) if isinstance(s, tuple)]
        op("s", out, ins, lambda e: e.activation(out[0], a[0], fn, bias=sc(bias), scale=sc(scale)))

    def mm(out, l, r, start=True, stop=True):
        op("t", out, [l, r], lambda e: e.matmul(out[0], l[0], r[0], start, stop))

    def iota(out, pattern, cm):
        op("g", out, [], lambda e: e.iota(out[0], pattern, 0, cm))

    def fill(out, c):
        op("v", out, [], lambda e: e.memset(out[0], c))

    def landed(ref, q, sem, n):
        for name, lo, hi in ref[1]:
            recs.setdefault(name, []).append((lo, hi, True, q, sem, n, {}))

    def load(q, out, src, sem):
        qobj[q].dma_start(out[0], src).then_inc(T.sem[sem], 16)
        landed(out, "dma", sem, 16)

    sends = [0]

    def send(to, out, src, sem):
        dst = T.cores[to]
        rid, pid = topo.addr(dst)[:2]
        access("g", src[1], [])
        g.remote_dma(out[0], src[0], T.sem[sem], T.sem["sent"], pid, rid, topo.mask(core, dst))
        sends[0] += len(topo.engines(core, dst))

    load("d", R("a0i"), T.a0[:, :], "la")
    load("s", R("hi0"), T.hd0[:, :], "lh0")
    load("s", R("fi0"), T.fl0[:, :], "lf0")
    load("d", R("sui", 0, 2048), T.su[:, :], "ls")
    load("s", R("za"), T.z0[:, :], "lz")
    load("d", R("xw"), T.xs[:, :], "lx")
    load("d", R("bank", B0, BD), T.gs[:, :], "lg")
    arrive = {}
    for t in range(ASKS):
        asker, asked = T.cores[(rank - 1 - t % (N - 1)) % N], T.cores[(rank + 1 + t % (N - 1)) % N]
        for n, sem, src in (("qpin", "rp", asker), ("zqin", "rz", asker), ("anin", "ra", asked)):
            arrive["%s%d" % (sem, t)] = len(topo.engines(src, core))
            landed(R("%s%d" % (n, t)), "rem", "%s%d" % (sem, t), len(topo.engines(src, core)))

    iota(R("ci"), [[1, 1]], 1)
    iota(R("ji"), [[1, 256]], 0)
    iota(R("sui", 2048, 4096), [[1, 2048]], 0)
    tc(R("pcol"), R("ci"))
    tc(R("jf"), R("ji"))
    ts(R("ci2"), R("ci"), 15, Op.bitwise_and)
    ts(R("ci3"), R("ci"), 4, Op.arith_shift_right)
    tc(R("p16"), R("ci2"))
    tc(R("pdiv"), R("ci3"))
    ts(R("jt"), R("ji"), 15, Op.bitwise_and)
    tc(R("pat16"), R("jt"))
    ts(R("mask16"), R("pat16"), R("p16"), Op.is_equal)
    tc(R("e16"), R("ji", 0, 16))
    ts(R("jt", 0, 128), R("ji", 0, 128), 4, Op.arith_shift_right)
    tc(R("qd16"), R("jt", 0, 128))
    ts(R("boh"), R("qd16"), R("pdiv"), Op.is_equal)
    ts(R("ob8h"), R("jf", 0, 8), R("pdiv"), Op.is_equal)
    ts(R("ob8k"), R("ob8h"), 1024.0, Op.mult)
    ts(R("maskm"), R("pat16"), R("p16"), Op.is_le, 4096.0, Op.mult)
    ts(R("ob8"), R("jf", 0, 8), R("pdiv"), Op.is_equal)
    ts(R("idb"), R("jf", 0, 128), R("pcol"), Op.is_equal)
    ts(R("lanb", 0, 8), R("jf", 0, 8), 0.0, Op.mult, R("pcol"), Op.add)
    ts(R("lanb", 8, 16), R("lanb", 0, 8), 128.0, Op.add)
    fill(R("ones"), 1.0)
    fill(R("zer"), 0.0)
    for j in range(16):
        actf(R("hm", 128 * j, 128 * j + 128), R("ones"), Fn.Copy, 0.0, R("mask16", j, j + 1))
    tc(R("als"), R("a0i"))
    tt(R("os"), IND(R("als"), R("e16")), R("mask16"), Op.mult)

    def spread(t):
        mm(R("ps1", 0, 256), R("boh"), R("os"))
        if t < STEPS:
            mm(R("ps3", 256, 512), R("boh"), R("os"), True, False)
            mm(R("ps3", 256, 512), R("idb"), R("maskm"), False, True)
            act(R("arm"), R("ps3", 256, 512))
        if t < ASKS:
            for h in (0, 1):
                o = R("ps1", 272 + 8 * h, 280 + 8 * h)
                mm(o, R("os", 128 * h, 128 * h + 128), R("ob8k"), True, False)
                mm(o, R("idb"), R("lanb", 8 * h, 8 * h + 8), False, True)

    spread(0)
    for c in range(15):
        if c != 7:
            fill(R("eb", 256 * c + 128 * (c >= 8), 272 * c + 16), 0.0)
    fill(R("bank", 0, B0), 0.0)
    ts(R("bo"), R("qd16"), R("pdiv"), Op.is_equal)
    ts(R("rpt"), R("idb"), 512.0, Op.mult)
    ts(R("cwt"), R("jf", 0, 128), R("pcol"), Op.is_gt)
    tt(R("cwt"), R("cwt"), R("rpt"), Op.subtract)
    ts(R("tri"), R("cwt"), 0.25, Op.mult)
    fill(R("quar"), 0.25)
    ts(R("ge8"), R("p16"), 8.0, Op.is_ge)
    ts(R("e8f"), R("jf", 0, 8), 2.0, Op.mult, R("ge8"), Op.add)
    tc(R("e8"), R("e8f"))
    ts(R("jt", 0, 128), R("ji", 0, 128), 7, Op.bitwise_and)
    ts(R("patc8"), R("jt", 0, 128), -32.0, Op.add)
    ts(R("jt", 0, 64), R("ji", 0, 64), 3, Op.arith_shift_right)
    ts(R("gm"), R("jt", 0, 64), R("pdiv"), Op.is_equal)
    ts(R("cwt"), R("hi0"), 33.0, Op.mult)
    ts(R("cw"), R("fi0"), 32.0, Op.mult)
    tt(R("cw"), R("cw"), R("cwt"), Op.add)

    def late_constants():
        ts(R("dump"), R("jf", 0, 8), 16.0, Op.mult, R("p16"), Op.add)
        ts(R("dump"), R("dump"), float(16 + 16384 - B0), Op.add)
        ts(R("is0"), R("pcol"), 0.0, Op.is_equal)
        ts(R("rowc"), R("pat16"), R("is0"), Op.mult)
        ts(R("om16"), R("ob8"), -16.0, Op.mult)
        ts(R("idn"), R("idb"), -1.0, Op.mult)
        ts(R("o16"), R("ob8"), 16.0, Op.mult)
        ts(R("o32"), R("ob8"), 32.0, Op.mult)
        ts(R("i128"), R("jf", 0, 128), 0.0, Op.add)
        ts(R("rpt"), R("pat16", 0, 128), 1.0, Op.add)
        tt(R("rpt"), R("rpt"), R("bo"), Op.mult)
        ts(R("rp"), R("rpt"), -1.0, Op.add)
        ts(R("odd"), R("p16"), 2.0, Op.mult, 1.0, Op.add)
        ts(R("bow"), R("bo"), R("odd"), Op.mult)
        ts(R("l16"), R("pcol"), 16.0, Op.mult)

    z = ["za", "zb"]

    def centres(a, b):
        for k in range(a, b):
            act(R("cc", 1024 * k, 1024 * k + 1024), IND(R("xw"), R("suu", 64 * k, 64 * k + 64)))

    def differences():
        for c in range(16):
            actf(R("rd", 128 * c, 128 * c + 128), R("i128"), Fn.Abs, R("alof", c, c + 1), 1.0)

    def head(t):
        tc(R("ai"), R("als"))
        tc(R("alu"), R("als"))
        ts(R("alo"), R("ai"), 127, Op.bitwise_and)
        if t > 0:
            tc(R("suu"), IND(R("sui", 0, 2048), R("alu")))
        tc(R("alou"), R("alo"))
        if t > 0:
            centres(0, 2)
        tc(R("arow"), R("ps1", 0, 256))
        mm(R("ps2", 0, 16), R("ones"), R("zer"), True, False)
        yield
        act(R("gc_"), IND(R("cw"), R("alou")))
        if t > 0:
            centres(2, 4)
        yield
        for c in range(15):
            ts(R("eb", 272 * c + 16, 256 * c + 256), R("arow", 16 * c + 16, 256), R("als", c, c + 1), Op.is_equal)
            for h in (0, 1) if c < 7 else (1,):
                mm(R("ps2", 8 * h, 8 * h + 8), R("eb", 256 * c + 128 * h, 256 * c + 128 * h + 128), R("ob8"), False, c == 14)
            yield
            if c == 6:
                tt(R("dg"), IND(R("als"), R("e16")), R("arm"), Op.is_equal)
                for h in (0, 1):
                    mm(R("ps2", 8 * h, 8 * h + 8), R("dg", 128 * h, 128 * h + 128), R("ob8"), False, False)
                yield
        if t == 0:
            tc(R("suu"), IND(R("sui", 0, 2048), R("alu")))
            centres(0, 4)
        tt(R("gmk"), IND(R("hm"), R("alu")), R("gc_"), Op.mult)
        for h in (0, 1):
            mm(R("ps7", 8 * h, 8 * h + 8), R("gmk", 128 * h, 128 * h + 128), R("ob8h"))
        yield
        ts(R("al4"), R("als"), 4.0, Op.mult, float(B0), Op.add)
        ts(R("ahi"), R("ai"), 7, Op.arith_shift_right)
        yield
        tc(R("cdi"), R("ps7", 0, 16))
        ts(R("alof"), R("alo"), -1.0, Op.mult)
        ts(R("hh"), R("cdi"), 31, Op.bitwise_and)
        ts(R("tl"), R("cdi"), 5, Op.arith_shift_right)
        tt(R("xx"), R("hh"), R("ps2", 0, 16), Op.add)
        tc(R("ahif"), R("ahi"))
        if t > 0:
            differences()
        yield
        tt(R("d1"), R("xx"), R("tl"), Op.subtract)
        ts(R("x3"), R("xx"), 3, Op.bitwise_and)
        ts(R("blk"), R("d1"), 0.0, Op.is_ge, 4.0, Op.mult)
        mm(R("ps2", 32, 40), R("tri"), R("blk", 0, 8))
        mm(R("ps2", 40, 48), R("tri"), R("blk", 8, 16), True, False)
        mm(R("ps2", 40, 48), R("quar"), R("blk", 0, 8), False, True)
        ts(R("s2"), R("d1"), 4.0, Op.is_lt)
        tt(R("y1"), R("x3"), R("blk"), Op.add)
        if t < ASKS:
            ts(R("pv1"), R("x3"), 256.0, Op.mult)
            tt(R("pv2"), R("pv1"), R("ps1", 272, 288), Op.add)
        yield
        ts(R("s1"), R("ps2", 32, 48), -384.0, Op.is_lt, 8.0, Op.mult)
        tt(R("p8"), R("s1"), R("s2"), Op.mult)
        tt(R("yv"), R("y1"), R("p8"), Op.add)
        yield
        tt(R("ay"), IND(R("yv"), R("e16")), R("mask16"), Op.mult)
        for h in (0, 1):
            mm(R("ps2", 48 + 8 * h, 56 + 8 * h), R("ay", 128 * h, 128 * h + 128), R("ob8"))
        yield

    def offsets(t):
        ts(R("pp"), R("ps2", 48, 64), 4.0, Op.is_lt)
        tt(R("oq"), R("ps2", 48, 64), R("al4"), Op.add)
        tt(R("offu"), R("oq"), R("pp"), Op.mult)
        yield
        ts(R("sb"), R("ps2", 48, 64), 4.0, Op.is_ge, 2048.0, Op.mult)
        tt(R("sou"), R("sb"), R("als"), Op.add)
        ts(R("pt"), R("ps2", 48, 64), 8.0, Op.is_ge, 32.0, Op.mult)
        tt(R("wl"), R("pp"), R("pt"), Op.add)
        yield

    made = [0]

    def onehot(c):
        if c >= made[0]:
            made[0] = c + 1
            ts(R("lh", 128 * c, 128 * c + 128), R("rp"), R("ahif", c, c + 1), Op.is_equal, R("wl", c, c + 1), Op.mult)

    def onehots(n):
        for _ in range(n):
            if made[0] < 16:
                onehot(made[0])

    def ask(t):
        to = (rank + 1 + t % (N - 1)) % N
        tc(R("ri"), R("ps2", 32, 48))
        ts(R("pv3"), R("p8"), 524288.0, Op.mult)
        tt(R("pv"), R("pv2"), R("pv3"), Op.add)
        ts(R("rlo"), R("ri"), 15, Op.bitwise_and)
        ts(R("rhi"), R("ri"), 4, Op.arith_shift_right)
        yield
        tt(R("cb"), IND(R("rhi"), R("e8")), R("patc8"), Op.is_equal)
        tt(R("ca"), IND(R("rlo"), R("e16")), R("pat16"), Op.is_equal)
        tt(R("cb2"), IND(R("pv"), R("e8")), R("cb"), Op.mult)
        for h in (0, 1):
            mm(R("ps5", 384, 448), R("ca", 128 * h, 128 * h + 128), R("cb2", 64 * h, 64 * h + 64), h == 0, h == 1)
        yield
        if t == 0:
            late_constants()
        else:
            onehots(8)
        qp = R("qp%d" % t)
        tt(R("cm"), R("ps5", 384, 448), R("gm"), Op.mult)
        tt(R("c1"), R("cm", 0, 32), R("cm", 32, 64), Op.add)
        tt(R("c2"), R("c1", 0, 16), R("c1", 16, 32), Op.add)
        tt(qp, R("c2", 0, 8), R("c2", 8, 16), Op.add)
        send(to, R("qpin%d" % t), qp, "rp%d" % t)
        ts(R("lni"), qp, 255, Op.bitwise_and)
        tc(R("lnu"), R("lni"))
        act(R("zq%d" % t), IND(R(z[0]), R("lnu")))
        send(to, R("zqin%d" % t), R("zq%d" % t), "rz%d" % t)
        yield
        ts(R("v1"), qp, 8, Op.arith_shift_right)
        tt(R("v2"), R("v1"), R("dump"), Op.max)
        ts(R("offr%d" % t), R("v2"), float(B0 - 16384), Op.add)
        yield

    def pops(t):
        if t > 0:
            wi, of, src = R("bank"), R("offr%d" % (t - 1)), R("anin%d" % (t - 1))
            op("v", (None, wi[1]), [src, of], lambda e: e.tensor_copy(wi[0].indirect(of[0]), src[0]))
        tt(R("zs"), IND(R("bank"), R("offu")), R(z[0]), Op.add)
        ts(R(z[1]), R("zs"), 0.0, Op.max, 255.0, Op.min)
        mm(R("ps3", 0, 256), R("ones"), R("rowc"), True, False)
        for h in (0, 1):
            for m in range(16 - NS):
                mm(R("ps3", 128 * h + m, 128 * h + 128, 16), R("cc", 2048 * h + m, 2048 * h + 2048, 16), R("om16"), False, False)
        for m in range(16 - NS, 16):
            mm(R(SBANK[m % NS], 0, 256), R("idb"), R("cc", m, 4096, 16), True, False)
        mm(R("ps4", 0, 256), R("idb"), R(z[1]))
        for m in range(16 - NS, 16):
            mm(R(SBANK[m % NS], 0, 256), R("idn"), R(z[1]), False, True)
            actf(R("mx", 256 * m, 256 * m + 256), R(SBANK[m % NS], 0, 256), Fn.Abs, 0.0, 1.0)
        tc(R("sp"), IND(R("sui"), R("sou")))
        if t == 0:
            differences()
        for c in range(0, 16, 4):
            actf(R("rh", 128 * c, 128 * c + 512), R("rd", 128 * c, 128 * c + 512), Fn.Relu, 1.0, -1.0)

    def update(t):
        for c in range(16):
            onehot(c)
            mm(R("ps5", 128, 256), R("lh", 128 * c, 128 * c + 128), R("rh", 128 * c, 128 * c + 128), c == 0, c == 15)
            yield

    def table():
        tt(R("cw"), R("cw"), R("ps5", 128, 256), Op.add)

    def dist(t):
        for m in range(16 - NS):
            tt(R("mx", 256 * m, 256 * m + 256), R("cc", m, 4096, 16), R("ps4", 0, 256), Op.max)
            for h in (0, 1):
                a = 256 * m + 128 * h
                mm(R("ps3", 128 * h + m, 128 * h + 128, 16), R("mx", a, a + 128), R("o32"), False, False)
            if m == 3:
                for n in range(16 - NS, 16):
                    for h in (0, 1):
                        mm(R("ps3", 128 * h + n, 128 * h + 128, 16), R(z[1], 128 * h, 128 * h + 128), R("o16"), False, False)
            if m == 15 - NS:
                for n in range(16 - NS, 16):
                    for h in (0, 1):
                        a = 256 * n + 128 * h
                        mm(R("ps3", 128 * h + n, 128 * h + 128, 16), R("mx", a, a + 128), R("o16"), False, h == 1 and n == 15)

    def choose(t):
        tc(R("ko"), R("ps3", 1, 256, 2))
        tt(R("k1"), R("ps3", 0, 256, 2), R("ko"), Op.min)
        act(R("ks"), R("ps3", 0, 256))
        yield
        src, w = "k1", 128
        for d in ("k2", "k3", "k4"):
            tt(R(d), R(src, 0, w, 2), R(src, 1, w, 2), Op.min)
            src, w = d, w // 2
            yield
        tt(R("oh"), IND(R("k4"), R("e16")), R("ks"), Op.is_equal)
        for h in (0, 1):
            mm(R("ps0", 256 + 128 * h, 384 + 128 * h), R("oh", 128 * h, 128 * h + 128), R("idb"))
        for _ in range(4):
            yield
        tt(R("os"), R("ps0", 256, 512), R("sp"), Op.mult)
        if t + 1 < STEPS:
            for h in (0, 1):
                mm(R("ps0", 128 * h, 128 * h + 128), R("os", 128 * h, 128 * h + 128), R("boh"))
            for _ in range(4):
                yield
            tt(R("aa"), R("ps0", 0, 256), R("mask16"), Op.mult)
            for h in (0, 1):
                mm(R("ps0", 256 + 8 * h, 264 + 8 * h), R("aa", 128 * h, 128 * h + 128), R("ob8h"))
        spread(t + 1)
        for _ in range(4):
            yield
        if t + 1 < STEPS:
            tc(R("als"), R("ps0", 256, 272))
        else:
            act(R("arf"), R("ps1", 0, 256))
        yield

    def answer(t):
        to = (rank - 1 - t % (N - 1)) % N
        qpin, zqin = R("qpin%d" % t), R("zqin%d" % t)
        ts(R("qa"), qpin, 10, Op.arith_shift_right, 2047, Op.bitwise_and)
        tc(R("qau"), R("qa"))
        act(R("goal"), IND(R("xw"), R("qau")))
        mm(R("ps5", 0, 128), R("bow"), zqin)
        mm(R("ps4", 256, 384), R("idn"), zqin, True, False)
        mm(R("ps4", 256, 384), R("idb"), R("goal"), False, True)
        tc(R("ui"), R("ps5", 0, 128))
        yield
        ts(R("uu"), R("ui"), 4095, Op.bitwise_and)
        yield
        tt(R("usq"), R("uu"), R("uu"), Op.mult)
        ts(R("um"), R("uu"), R("odd"), Op.mult)
        yield
        ts(R("uv"), R("usq"), 5, Op.arith_shift_right)
        yield
        tt(R("us"), R("um"), R("uv"), Op.add)
        yield
        ts(R("ux"), R("us"), 8191, Op.bitwise_and)
        yield
        tc(R("cou"), R("ux"))
        for k in range(2):
            act(R("cand", 1024 * k, 1024 * k + 1024), IND(R("bank", B0, BD), R("cou", 64 * k, 64 * k + 64)))
        yield "gathering"
        mm(R("ps6", 0, 128), R("ones"), R("rowc", 0, 128), True, False)
        for m in range(16):
            mm(R("ps6", m, 128, 16), R("cand", m, 2048, 16), R("om16"), False, False)
        for m in range(16):
            tt(R("mq", 128 * m, 128 * m + 128), R("cand", m, 2048, 16), R("ps4", 256, 384), Op.max)
            mm(R("ps6", m, 128, 16), R("mq", 128 * m, 128 * m + 128), R("o32"), False, m == 15)
            yield
        tc(R("q0"), R("ps6", 1, 128, 2))
        tt(R("q1"), R("ps6", 0, 128, 2), R("q0"), Op.min)
        src, w = "q1", 64
        for d in ("q2", "q3", "q4"):
            yield
            tt(R(d), R(src, 0, w, 2), R(src, 1, w, 2), Op.min)
            src, w = d, w // 2
        yield
        ts(R("q5"), R("q4"), 15, Op.bitwise_and)
        yield
        ts(R("q6"), R("q5"), R("l16"), Op.add)
        yield
        tt(R("aq"), IND(R("q6"), R("e16", 0, 8)), R("mask16", 0, 128), Op.mult)
        mm(R("ps5", 448, 456), R("aq"), R("ob8h"))
        yield
        tc(R("seu"), R("ps5", 448, 456))
        yield
        tc(R("an%d" % t), IND(R("cand"), R("seu")))
        send(to, R("anin%d" % t), R("an%d" % t), "ra%d" % t)
        yield

    def finish(t):
        for _ in update(t):
            yield
        for _ in range(3):
            yield
        table()
        ts(R("w1"), R("cw"), 1.0, Op.mult)
        yield
        ts(R("w2"), R("w1"), 31, Op.bitwise_and)
        ts(R("w3"), R("w1"), 5, Op.arith_shift_right)
        ts(R("w4"), R("w1"), 3, Op.bitwise_and)
        yield
        tt(R("oyf"), R("w3"), R("w2"), Op.subtract)
        tc(R("ohf"), R("w4"))
        yield

    def run(gen):
        for _ in gen:
            pass

    def until(x, tag):
        for y in x:
            yield
            if y == tag:
                return

    def weave(*gens):
        gens = list(gens)
        while gens:
            for x in list(gens):
                if x in gens and next(x, "end") == "end":
                    gens = [y for y in gens if y is not x]

    nothing = iter(())
    run(head(0))
    for t in range(STEPS):
        asks, more = t < ASKS, t + 1 < STEPS
        weave(offsets(t), ask(t) if asks else nothing)
        pops(t)
        dist(t)
        ch, ans = choose(t), answer(t) if asks else nothing
        onehots(4)
        next(ch)
        if more:
            weave(until(ans, "gathering"), ch, update(t))
            nxt = head(t + 1)
            next(nxt)
            table()
            for _ in range(5):
                next(nxt)
            weave(ans, nxt, ans)
        else:
            weave(finish(t), ch)
        made[0] = 0
        z.reverse()

    outs = [0]

    def store(dst, ap, ref):
        access("d", ref[1], [])
        g.sync.dma_start(dst, ap).then_inc(T.sem["sout"], 16)
        outs[0] += 16

    store(T.yz[:, :], R(z[0])[0], R(z[0]))
    buf, base, w = PACK["arf"]
    store(T.ya[:, :], T[buf][0:128:16, base:base + w], R("arf"))
    store(T.yf[:, :], R("oyf")[0], R("oyf"))
    store(T.yh[:, :], R("ohf")[0], R("ohf"))
    g.sync.wait_ge(T.sem["sout"], outs[0])
    for q in "vstg":
        need("g", qsem[q], count[q], {})
    for s in LOADS:
        need("g", s, 16, {})
    for s in sorted(arrive):
        need("g", s, arrive[s], {})
    g.wait_ge(T.sem["sent"], sends[0])
